import numpy as np
import ml_dtypes


def mxq(x, axis, fmt="e4m3"):
    dtype, down = {"e4m3": (ml_dtypes.float8_e4m3fn, 7), "e5m2": (ml_dtypes.float8_e5m2, 14)}[fmt]
    v = np.moveaxis(np.asarray(x, np.float32).astype(ml_dtypes.bfloat16).astype(np.float64), axis, -1)
    blocks = v.reshape(v.shape[:-1] + (-1, 32))
    amax = np.abs(blocks).max(-1, keepdims=True)
    byte = np.maximum(np.where(amax > 0, np.frexp(amax)[1] - 1 + 127, 0) - down, 1)
    scale = np.exp2(byte - 127.0)
    codes = (blocks / scale).astype(np.float32).astype(dtype).astype(np.float64)
    return np.moveaxis((codes * scale).reshape(v.shape), -1, axis)


WIDE = False


def mx_kscale(k):
    if not WIDE:
        return np.ones(k)
    levels = np.array([10, -10, 5, -5, 0])
    if k % 512:
        return np.exp2(np.random.permutation(np.resize(levels, k // 32))).repeat(32)
    a = np.empty((k // 512, 16))
    for p in range(k // 512):
        a[p, :8] = np.random.permutation(np.resize(levels, 8))
        for g in range(8):
            far = levels[np.abs(levels - a[p, g]) >= 10]
            a[p, g + 8] = far[np.random.randint(len(far))]
    return np.exp2(a.ravel()).repeat(32)


def f64(x):
    return np.asarray(x).astype(np.float64)


def striped(idx):
    return np.tile(idx.reshape(-1, 16).T, (8, 1)).astype(np.uint16)


def unstriped(offs):
    return offs[:16].T.reshape(-1).astype(np.int64)


K, T, E, C, N = 1536, 1024, 8, 256, 128


def by_expert(wq, xq):
    return np.concatenate([wq[e].T @ xq[:, e * C:(e + 1) * C] for e in range(E)], axis=1)


def setup_inputs():
    n = np.random.standard_normal
    s = mx_kscale(K)[:, None]
    first = np.random.permutation(np.repeat(np.arange(E), T // E))
    second = (first + 1 + np.random.permutation(np.repeat(np.arange(E - 1), -(-T // (E - 1)))[:T])) % E
    while np.bincount(second, minlength=E).max() != T // E:
        load = np.bincount(second, minlength=E); hi, lo = int(load.argmax()), int(load.argmin())
        t = np.flatnonzero((second == hi) & (first != lo))[0]; second[t] = lo
    slot_token = np.empty(E * C, np.int64); pos = np.empty((2, T), np.int64); fill = np.zeros(E, np.int64)
    place = np.stack([np.random.permutation(C) for _ in range(E)])
    for r, deal in enumerate((first, second)):
        for t in np.random.permutation(T):
            e = deal[t]; j = e * C + place[e, fill[e]]; fill[e] += 1; slot_token[j] = t; pos[r, t] = j
    g = np.random.uniform(0.2, 0.8, T)
    return {
        "xT": (n((K, T)) * s).astype(np.float32),
        "w": (n((E, K, N)) / np.sqrt(K) / s[None]).astype(np.float32),
        "gate": np.stack([np.tile(g, (N, 1)), np.tile(1.0 - g, (N, 1))]).astype(np.float32),
        "offs": striped(slot_token),
        "pos1": striped(pos[0]),
        "pos2": striped(pos[1]),
    }


def reference(xT, w, gate, offs, pos1, pos2):
    idx = unstriped(offs)
    xq = mxq(f64(xT)[:, idx], 0, "e4m3")
    y = by_expert(mxq(f64(w), 1, "e4m3"), xq)
    return f64(gate[0]) * y[:, unstriped(pos1)] + f64(gate[1]) * y[:, unstriped(pos2)]

@@ -1,0 +1,177 @@
+from contextlib import ExitStack
+
+import concourse.mybir as mybir
+
+K, T, E, C, N = 1536, 1024, 8, 256, 128
+FLOPS = 2 * K * N * E * C
+
+F32 = mybir.dt.float32
+BF16 = mybir.dt.bfloat16
+U32 = mybir.dt.uint32
+U16 = mybir.dt.uint16
+U8 = mybir.dt.uint8
+FP8X4 = mybir.dt.float8_e4m3fn_x4
+MULT = mybir.AluOpType.mult
+ADD = mybir.AluOpType.add
+
+P = 128
+PASSES = K // 512
+UNITS = E * PASSES
+
+
+def tile_routed_moe_kernel(tc, xT, w, gate, offs, pos1, pos2, out):
+    nc = tc.nc
+    with ExitStack() as ctx:
+        keep = ctx.enter_context(tc.tile_pool(name="keep", bufs=1))
+        psum = ctx.enter_context(tc.psum_pool(name="psum", bufs=1))
+
+        offs_sb = keep.tile([P, E * C // 16], U16, name="offs_sb")
+        pos1_sb = keep.tile([P, T // 16], U16, name="pos1_sb")
+        pos2_sb = keep.tile([P, T // 16], U16, name="pos2_sb")
+
+        x_view = xT.rearrange("(a p j) n -> a p j n", p=P, j=4)
+        w_view = w.rearrange("e (a p j) n -> p (e a) j n", p=P, j=4)
+
+        chunks = [(0, 0, 256, "s"), (0, 256, 256, "s"), (0, 512, 256, "v"), (0, 768, 256, "v")]
+        gpsimd_chunks = (0, 2)
+        for a in (1, 2):
+            chunks += [(a, 0, 512, "s"), (a, 512, 512, "s")]
+        w_chunks = [(0, 4), (4, 4), (8, 4), (12, 4), (16, 4), (20, 2), (22, 2)]
+
+        x_raw = []
+        for i, (a, t0, n, eng) in enumerate(chunks):
+            raw = keep.tile([P, 4, n], F32, name=f"x_raw{i}")
+            nc.sync.dma_start(out=raw[:], in_=x_view[a, :, :, t0 : t0 + n])
+            x_raw.append(raw)
+            if i == 1:
+                nc.sync.dma_start(offs_sb[:], offs)
+        w_raw = []
+        for i, (u0, n) in enumerate(w_chunks):
+            raw = keep.tile([P, n, 4, N], F32, name=f"w_raw{i}", tag="late" if i == len(w_chunks) - 1 else f"w_raw{i}")
+            nc.sync.dma_start(out=raw[:], in_=w_view[:, u0 : u0 + n, :, :])
+            w_raw.append(raw)
+        nc.sync.dma_start(pos1_sb[:], pos1)
+        nc.sync.dma_start(pos2_sb[:], pos2)
+        gates = []
+        for r in range(2):
+            g = keep.tile([P, T], F32, name=f"gate{r}")
+            nc.sync.dma_start(out=g[:], in_=gate[r, :, :])
+            gates.append(g)
+
+        words = [keep.tile([P, T], U32, align_bytes=64, name=f"words{a}") for a in range(PASSES)]
+        planes = keep.tile([P, T], U8, align_bytes=64, name="planes")
+        nc.gpsimd.memset(planes[:], 0)
+
+        slot_words = keep.tile([P, PASSES, E * C], U32, align_bytes=64, name="slot_words")
+        slot_planes = keep.tile([P, E * C], U8, align_bytes=64, name="slot_planes")
+        w_codes = keep.tile([P, UNITS, N], U32, align_bytes=64, name="w_codes")
+        w_scales = keep.tile([P, UNITS, N], U8, align_bytes=64, name="w_scales")
+
+        def copy(eng, dst, src):
+            if eng == "v":
+                nc.vector.tensor_copy(out=dst, in_=src)
+            elif eng == "g":
+                nc.gpsimd.tensor_copy(out=dst, in_=src)
+            else:
+                nc.scalar.copy(out=dst, in_=src)
+
+        x_grouped = []
+        for i, (a, t0, n, eng) in enumerate(chunks):
+            grouped = keep.tile([P, n * 4], BF16, align_bytes=64, name=f"x_grouped{i}")
+            copy(
+                eng,
+                grouped[:].rearrange("p (c i j) -> p c j i", i=4, j=4),
+                x_raw[i][:].rearrange("p j (c i) -> p c j i", i=4),
+            )
+            x_grouped.append(grouped)
+        w_grouped = []
+        for i, (u0, n) in enumerate(w_chunks):
+            grouped = keep.tile([P, n * N * 4], BF16, align_bytes=64, name=f"w_grouped{i}")
+            if i in gpsimd_chunks:
+                for u in range(n):
+                    nc.gpsimd.tensor_scalar(
+                        out=grouped[:, u * 4 * N : (u + 1) * 4 * N].rearrange("p (c i j) -> p c j i", i=4, j=4),
+                        in0=w_raw[i][:, u, :, :].rearrange("p j (c i) -> p c j i", i=4),
+                        scalar1=1.0,
+                        scalar2=0.0,
+                        op0=MULT,
+                        op1=ADD,
+                    )
+            else:
+                nc.scalar.copy(
+                    out=grouped[:].rearrange("p (u c i j) -> p u c j i", u=n, i=4, j=4),
+                    in_=w_raw[i][:].rearrange("p u j (c i) -> p u c j i", i=4),
+                )
+            w_grouped.append(grouped)
+
+        def tokens(i):
+            a, t0, n, eng = chunks[i]
+            nc.vector.quantize_mx(
+                out=words[a][:, t0 : t0 + n].bitcast(FP8X4),
+                scales=planes[4 * a : P, t0 : t0 + n],
+                in_=x_grouped[i][:],
+            )
+
+        def gather_words(a, cuts):
+            for s, n in cuts:
+                nc.vector.tensor_copy(
+                    out=slot_words[:, a, s : s + n],
+                    in_=words[a][:].indirect(offs_sb[:, s // 16 : (s + n) // 16]),
+                )
+
+        def weights(i):
+            u0, n = w_chunks[i]
+            nc.vector.quantize_mx(
+                out=w_codes[:, u0 : u0 + n, :].rearrange("p u n -> p (u n)").bitcast(FP8X4),
+                scales=w_scales[:, u0 : u0 + n, :].rearrange("p u n -> p (u n)"),
+                in_=w_grouped[i][:],
+            )
+
+        THREE = [(0, 768), (768, 768), (1536, 512)]
+        FOUR = [(0, 768), (768, 768), (1536, 256), (1792, 256)]
+        for i in range(4):
+            tokens(i)
+        gather_words(0, THREE)
+        tokens(4)
+        tokens(5)
+        gather_words(1, THREE)
+        tokens(6)
+        tokens(7)
+        for s, n in THREE:
+            nc.vector.tensor_copy(
+                out=slot_planes[:, s : s + n],
+                in_=planes[:].indirect(offs_sb[:, s // 16 : (s + n) // 16]),
+            )
+        for i in range(len(w_chunks)):
+            weights(i)
+        gather_words(2, FOUR)
+
+        y = keep.tile([P, E * C], F32, name="y", tag="late")
+        accs = [psum.tile([P, C], F32, name=f"acc{e}") for e in range(E)]
+        for a in range(PASSES):
+            for e in range(E):
+                acc = accs[e]
+                cols = slice(e * C, (e + 1) * C)
+                u = e * PASSES + a
+                nc.tensor.matmul_mx(
+                    out=acc[:],
+                    lhsT=w_codes[:, u, :].bitcast(FP8X4),
+                    lhsT_scale=w_scales[:, u, :],
+                    rhs=slot_words[:, a, cols].bitcast(FP8X4),
+                    rhs_scale=slot_planes[4 * a : P, cols],
+                    start=(a == 0),
+                    stop=(a == PASSES - 1),
+                )
+                if a == PASSES - 1:
+                    nc.scalar.copy(out=y[:, cols], in_=acc[:])
+
+        for i, (t0, n) in enumerate([(0, 768), (768, 256)]):
+            first = keep.tile([P, n], F32, name=f"first{i}")
+            second = keep.tile([P, n], F32, name=f"second{i}")
+            total = keep.tile([P, n], F32, name=f"total{i}")
+            for dst, pos_sb, g in ((first, pos1_sb, gates[0]), (second, pos2_sb, gates[1])):
+                nc.vector.tensor_tensor(
+                    dst[:], y[:].indirect(pos_sb[:, t0 // 16 : (t0 + n) // 16]), g[:, t0 : t0 + n], MULT
+                )
+            nc.vector.tensor_tensor(total[:], first[:], second[:], ADD)
+            nc.sync.dma_start(out=out[:, t0 : t0 + n], in_=total[:])

@@ -17,12 +17,15 @@ ADD = mybir.AluOpType.add
 P = 128
 PASSES = K // 512
 UNITS = E * PASSES
+SLOTS = E * C
+WIDE = 2 * SLOTS
 
 
 def tile_routed_moe_kernel(tc, xT, w, gate, offs, pos1, pos2, out):
     nc = tc.nc
     with ExitStack() as ctx:
         keep = ctx.enter_context(tc.tile_pool(name="keep", bufs=1))
+        late = ctx.enter_context(tc.tile_pool(name="late", bufs=1))
         psum = ctx.enter_context(tc.psum_pool(name="psum", bufs=1))
 
         offs_sb = keep.tile([P, E * C // 16], U16, name="offs_sb")
@@ -32,22 +35,26 @@ def tile_routed_moe_kernel(tc, xT, w, gate, offs, pos1, pos2, out):
         x_view = xT.rearrange("(a p j) n -> a p j n", p=P, j=4)
         w_view = w.rearrange("e (a p j) n -> p (e a) j n", p=P, j=4)
 
-        chunks = [(0, 0, 256, "s"), (0, 256, 256, "s"), (0, 512, 256, "v"), (0, 768, 256, "v")]
-        gpsimd_chunks = (0, 2)
-        for a in (1, 2):
-            chunks += [(a, 0, 512, "s"), (a, 512, 512, "s")]
-        w_chunks = [(0, 4), (4, 4), (8, 4), (12, 4), (16, 4), (20, 2), (22, 2)]
+        chunks = [(0, 0, 256, 0), (0, 256, 256, 0), (0, 512, 256, 256), (0, 768, 256, 160)]
+        chunks += [(1, t0, 256, 0) for t0 in range(0, T, 256)]
+        chunks += [(2, 0, 512, 0), (2, 512, 512, 0)]
+        w_chunks = [(u0, 4, 1) for u0 in range(0, 20, 4)] + [(20, 2, 0), (22, 2, 0)]
+        x_calls = [[0], [1], [2], [3], [4, 5], [6, 7], [8], [9]]
+        w_calls = [[0, 1], [2, 3], [4], [5, 6]]
 
         x_raw = []
-        for i, (a, t0, n, eng) in enumerate(chunks):
+        for i, (a, t0, n, nv) in enumerate(chunks):
             raw = keep.tile([P, 4, n], F32, name=f"x_raw{i}")
             nc.sync.dma_start(out=raw[:], in_=x_view[a, :, :, t0 : t0 + n])
             x_raw.append(raw)
-            if i == 1:
+            if i == 3:
                 nc.sync.dma_start(offs_sb[:], offs)
         w_raw = []
-        for i, (u0, n) in enumerate(w_chunks):
-            raw = keep.tile([P, n, 4, N], F32, name=f"w_raw{i}", tag="late" if i == len(w_chunks) - 1 else f"w_raw{i}")
+        for i, (u0, n, ng) in enumerate(w_chunks):
+            if i == len(w_chunks) - 1:
+                raw = late.tile([P, n, 4, N], F32, align_bytes=64, offset=0, name=f"w_raw{i}")
+            else:
+                raw = keep.tile([P, n, 4, N], F32, align_bytes=64, name=f"w_raw{i}")
             nc.sync.dma_start(out=raw[:], in_=w_view[:, u0 : u0 + n, :, :])
             w_raw.append(raw)
         nc.sync.dma_start(pos1_sb[:], pos1)
@@ -58,112 +65,119 @@ def tile_routed_moe_kernel(tc, xT, w, gate, offs, pos1, pos2, out):
             nc.sync.dma_start(out=g[:], in_=gate[r, :, :])
             gates.append(g)
 
-        words = [keep.tile([P, T], U32, align_bytes=64, name=f"words{a}") for a in range(PASSES)]
-        planes = keep.tile([P, T], U8, align_bytes=64, name="planes")
-        nc.gpsimd.memset(planes[:], 0)
+        words = keep.tile([P, (PASSES - 1) * T + WIDE], U32, align_bytes=64, name="words")
+        planes = keep.tile([P, WIDE], U8, align_bytes=64, name="planes")
+        nc.gpsimd.memset(planes[:, 0:T], 0)
 
-        slot_words = keep.tile([P, PASSES, E * C], U32, align_bytes=64, name="slot_words")
-        slot_planes = keep.tile([P, E * C], U8, align_bytes=64, name="slot_planes")
+        def first_word(a):
+            return (PASSES - 1 - a) * T
+
+        early_words = keep.tile([P, PASSES - 1, SLOTS], U32, align_bytes=64, name="early_words")
+        slot_planes = keep.tile([P, SLOTS], U8, align_bytes=64, name="slot_planes")
         w_codes = keep.tile([P, UNITS, N], U32, align_bytes=64, name="w_codes")
         w_scales = keep.tile([P, UNITS, N], U8, align_bytes=64, name="w_scales")
 
-        def copy(eng, dst, src):
-            if eng == "v":
-                nc.vector.tensor_copy(out=dst, in_=src)
-            elif eng == "g":
-                nc.gpsimd.tensor_copy(out=dst, in_=src)
-            else:
-                nc.scalar.copy(out=dst, in_=src)
-
         x_grouped = []
-        for i, (a, t0, n, eng) in enumerate(chunks):
-            grouped = keep.tile([P, n * 4], BF16, align_bytes=64, name=f"x_grouped{i}")
-            copy(
-                eng,
-                grouped[:].rearrange("p (c i j) -> p c j i", i=4, j=4),
-                x_raw[i][:].rearrange("p j (c i) -> p c j i", i=4),
-            )
+        for k, call in enumerate(x_calls):
+            grouped = keep.tile([P, sum(chunks[i][2] for i in call) * 4], BF16, align_bytes=64, name=f"x_grouped{k}")
+            for i in call:
+                a, t0, n, nv = chunks[i]
+                c0 = (t0 - chunks[call[0]][1]) * 4
+                dst = grouped[:, c0 : c0 + 4 * n].rearrange("p (c i j) -> p c j i", i=4, j=4)
+                src = x_raw[i][:].rearrange("p j (c i) -> p c j i", i=4)
+                if nv:
+                    nc.vector.tensor_copy(out=dst[:, 0 : nv // 4, :, :], in_=src[:, 0 : nv // 4, :, :])
+                if nv < n:
+                    nc.scalar.copy(out=dst[:, nv // 4 : n // 4, :, :], in_=src[:, nv // 4 : n // 4, :, :])
             x_grouped.append(grouped)
         w_grouped = []
-        for i, (u0, n) in enumerate(w_chunks):
-            grouped = keep.tile([P, n * N * 4], BF16, align_bytes=64, name=f"w_grouped{i}")
-            if i in gpsimd_chunks:
-                for u in range(n):
+        for k, call in enumerate(w_calls):
+            grouped = keep.tile(
+                [P, sum(w_chunks[i][1] for i in call) * 4 * N], BF16, align_bytes=64, name=f"w_grouped{k}"
+            )
+            for i in call:
+                u0, n, ng = w_chunks[i]
+                c0 = (u0 - w_chunks[call[0]][0]) * 4 * N
+                ns = n - ng
+                nc.scalar.copy(
+                    out=grouped[:, c0 : c0 + ns * 4 * N].rearrange("p (u c i j) -> p u c j i", u=ns, i=4, j=4),
+                    in_=w_raw[i][:, 0:ns, :, :].rearrange("p u j (c i) -> p u c j i", i=4),
+                )
+                for u in range(ns, n):
                     nc.gpsimd.tensor_scalar(
-                        out=grouped[:, u * 4 * N : (u + 1) * 4 * N].rearrange("p (c i j) -> p c j i", i=4, j=4),
+                        out=grouped[:, c0 + u * 4 * N : c0 + (u + 1) * 4 * N].rearrange(
+                            "p (c i j) -> p c j i", i=4, j=4
+                        ),
                         in0=w_raw[i][:, u, :, :].rearrange("p j (c i) -> p c j i", i=4),
                         scalar1=1.0,
                         scalar2=0.0,
                         op0=MULT,
                         op1=ADD,
                     )
-            else:
-                nc.scalar.copy(
-                    out=grouped[:].rearrange("p (u c i j) -> p u c j i", u=n, i=4, j=4),
-                    in_=w_raw[i][:].rearrange("p u j (c i) -> p u c j i", i=4),
-                )
             w_grouped.append(grouped)
 
-        def tokens(i):
-            a, t0, n, eng = chunks[i]
+        def tokens(k):
+            a, t0 = chunks[x_calls[k][0]][0:2]
+            n = sum(chunks[i][2] for i in x_calls[k])
             nc.vector.quantize_mx(
-                out=words[a][:, t0 : t0 + n].bitcast(FP8X4),
+                out=words[:, first_word(a) + t0 : first_word(a) + t0 + n].bitcast(FP8X4),
                 scales=planes[4 * a : P, t0 : t0 + n],
-                in_=x_grouped[i][:],
+                in_=x_grouped[k][:],
             )
 
-        def gather_words(a, cuts):
-            for s, n in cuts:
-                nc.vector.tensor_copy(
-                    out=slot_words[:, a, s : s + n],
-                    in_=words[a][:].indirect(offs_sb[:, s // 16 : (s + n) // 16]),
-                )
+        def gather(dst, window, s, n):
+            nc.vector.tensor_copy(out=dst, in_=window.indirect(offs_sb[:, s // 16 : (s + n) // 16]))
 
-        def weights(i):
-            u0, n = w_chunks[i]
+        def weights(k):
+            u0 = w_chunks[w_calls[k][0]][0]
+            n = sum(w_chunks[i][1] for i in w_calls[k])
             nc.vector.quantize_mx(
                 out=w_codes[:, u0 : u0 + n, :].rearrange("p u n -> p (u n)").bitcast(FP8X4),
                 scales=w_scales[:, u0 : u0 + n, :].rearrange("p u n -> p (u n)"),
-                in_=w_grouped[i][:],
+                in_=w_grouped[k][:],
             )
 
-        THREE = [(0, 768), (768, 768), (1536, 512)]
-        FOUR = [(0, 768), (768, 768), (1536, 256), (1792, 256)]
-        for i in range(4):
-            tokens(i)
-        gather_words(0, THREE)
-        tokens(4)
-        tokens(5)
-        gather_words(1, THREE)
-        tokens(6)
-        tokens(7)
-        for s, n in THREE:
-            nc.vector.tensor_copy(
-                out=slot_planes[:, s : s + n],
-                in_=planes[:].indirect(offs_sb[:, s // 16 : (s + n) // 16]),
-            )
-        for i in range(len(w_chunks)):
-            weights(i)
-        gather_words(2, FOUR)
-
-        y = keep.tile([P, E * C], F32, name="y", tag="late")
-        accs = [psum.tile([P, C], F32, name=f"acc{e}") for e in range(E)]
         for a in range(PASSES):
-            for e in range(E):
-                acc = accs[e]
-                cols = slice(e * C, (e + 1) * C)
+            for k in range(len(x_calls)):
+                if chunks[x_calls[k][0]][0] == a:
+                    tokens(k)
+            if a < PASSES - 1:
+                gather(early_words[:, a, :], words[:, first_word(a) : first_word(a) + WIDE], 0, SLOTS)
+        gather(slot_planes[:], planes[:], 0, SLOTS)
+
+        last_window = words[:, 0 : 2 * T]
+        weights(0)
+        late_a = keep.tile([P, 4 * C], U32, align_bytes=64, name="late_a", tag="w_raw1")
+        gather(late_a[:], last_window, 0, 4 * C)
+        weights(1)
+        weights(2)
+        late_b = keep.tile([P, 3 * C], U32, align_bytes=64, name="late_b", tag="w_raw4")
+        gather(late_b[:], last_window, 4 * C, 3 * C)
+        weights(3)
+        late_c = late.tile([P, C], U32, align_bytes=64, offset=0, name="late_c")
+        gather(late_c[:], last_window, 7 * C, C)
+        last_words = [late_a[:, e * C : (e + 1) * C] for e in range(4)]
+        last_words += [late_b[:, e * C : (e + 1) * C] for e in range(3)] + [late_c[:]]
+
+        accs = [psum.tile([P, C], F32, name=f"acc{e}") for e in range(E)]
+        for e in range(E):
+            for a in range(PASSES):
                 u = e * PASSES + a
+                cols = slice(e * C, (e + 1) * C)
+                rhs = last_words[e] if a == PASSES - 1 else early_words[:, a, cols]
                 nc.tensor.matmul_mx(
-                    out=acc[:],
+                    out=accs[e][:],
                     lhsT=w_codes[:, u, :].bitcast(FP8X4),
                     lhsT_scale=w_scales[:, u, :],
-                    rhs=slot_words[:, a, cols].bitcast(FP8X4),
+                    rhs=rhs.bitcast(FP8X4),
                     rhs_scale=slot_planes[4 * a : P, cols],
                     start=(a == 0),
                     stop=(a == PASSES - 1),
                 )
-                if a == PASSES - 1:
-                    nc.scalar.copy(out=y[:, cols], in_=acc[:])
+
+        y = late.tile([P, SLOTS], F32, align_bytes=64, offset=4 * C, name="y")
+        for e in range(E):
+            nc.scalar.copy(out=y[:, e * C : (e + 1) * C], in_=accs[e][:])
 
         for i, (t0, n) in enumerate([(0, 768), (768, 256)]):
             first = keep.tile([P, n], F32, name=f"first{i}")

@@ -35,19 +35,20 @@ def tile_routed_moe_kernel(tc, xT, w, gate, offs, pos1, pos2, out):
         x_view = xT.rearrange("(a p j) n -> a p j n", p=P, j=4)
         w_view = w.rearrange("e (a p j) n -> p (e a) j n", p=P, j=4)
 
-        chunks = [(0, 0, 256, 0), (0, 256, 256, 0), (0, 512, 256, 256), (0, 768, 256, 160)]
-        chunks += [(1, t0, 256, 0) for t0 in range(0, T, 256)]
-        chunks += [(2, 0, 512, 0), (2, 512, 512, 0)]
+        x_loads = [(0, 0, 512), (0, 512, 256), (0, 768, 256)]
+        x_loads += [(a, t0, 512) for a in (1, 2) for t0 in (0, 512)]
+        x_calls = [(0, 0, 256, 256), (0, 256, 256, 0), (0, 512, 256, 64), (0, 768, 256, 192)]
+        x_calls += [(1, 0, 512, 0), (1, 512, 512, 160), (2, 0, 512, 0), (2, 512, 512, 0)]
         w_chunks = [(u0, 4, 1) for u0 in range(0, 20, 4)] + [(20, 2, 0), (22, 2, 0)]
-        x_calls = [[0], [1], [2], [3], [4, 5], [6, 7], [8], [9]]
         w_calls = [[0, 1], [2, 3], [4], [5, 6]]
 
-        x_raw = []
-        for i, (a, t0, n, nv) in enumerate(chunks):
+        x_raw = {}
+        for i, (a, t0, n) in enumerate(x_loads):
             raw = keep.tile([P, 4, n], F32, name=f"x_raw{i}")
             nc.sync.dma_start(out=raw[:], in_=x_view[a, :, :, t0 : t0 + n])
-            x_raw.append(raw)
-            if i == 3:
+            for t in range(t0, t0 + n, 128):
+                x_raw[(a, t)] = raw[:, :, t - t0 : n]
+            if i == 2:
                 nc.sync.dma_start(offs_sb[:], offs)
         w_raw = []
         for i, (u0, n, ng) in enumerate(w_chunks):
@@ -77,19 +78,24 @@ def tile_routed_moe_kernel(tc, xT, w, gate, offs, pos1, pos2, out):
         w_codes = keep.tile([P, UNITS, N], U32, align_bytes=64, name="w_codes")
         w_scales = keep.tile([P, UNITS, N], U8, align_bytes=64, name="w_scales")
 
-        x_grouped = []
-        for k, call in enumerate(x_calls):
-            grouped = keep.tile([P, sum(chunks[i][2] for i in call) * 4], BF16, align_bytes=64, name=f"x_grouped{k}")
-            for i in call:
-                a, t0, n, nv = chunks[i]
-                c0 = (t0 - chunks[call[0]][1]) * 4
-                dst = grouped[:, c0 : c0 + 4 * n].rearrange("p (c i j) -> p c j i", i=4, j=4)
-                src = x_raw[i][:].rearrange("p j (c i) -> p c j i", i=4)
-                if nv:
-                    nc.vector.tensor_copy(out=dst[:, 0 : nv // 4, :, :], in_=src[:, 0 : nv // 4, :, :])
-                if nv < n:
-                    nc.scalar.copy(out=dst[:, nv // 4 : n // 4, :, :], in_=src[:, nv // 4 : n // 4, :, :])
-            x_grouped.append(grouped)
+        def gather(dst, window, s, n):
+            nc.vector.tensor_copy(out=dst, in_=window.indirect(offs_sb[:, s // 16 : (s + n) // 16]))
+
+        for k, (a, t0, n, nv) in enumerate(x_calls):
+            grouped = keep.tile([P, n * 4], BF16, align_bytes=64, name=f"x_grouped{k}", tag=f"x_grouped{k % 2 if a == 0 else k}")
+            dst = grouped[:].rearrange("p (c i j) -> p c j i", i=4, j=4)
+            src = x_raw[(a, t0)][:, :, 0:n].rearrange("p j (c i) -> p c j i", i=4)
+            if nv:
+                nc.vector.tensor_copy(out=dst[:, 0 : nv // 4, :, :], in_=src[:, 0 : nv // 4, :, :])
+            if nv < n:
+                nc.scalar.copy(out=dst[:, nv // 4 : n // 4, :, :], in_=src[:, nv // 4 : n // 4, :, :])
+            nc.vector.quantize_mx(
+                out=words[:, first_word(a) + t0 : first_word(a) + t0 + n].bitcast(FP8X4),
+                scales=planes[4 * a : P, t0 : t0 + n],
+                in_=grouped[:],
+            )
+            if t0 + n == T and a < PASSES - 1:
+                gather(early_words[:, a, :], words[:, first_word(a) : first_word(a) + WIDE], 0, SLOTS)
         w_grouped = []
         for k, call in enumerate(w_calls):
             grouped = keep.tile(
@@ -116,18 +122,6 @@ def tile_routed_moe_kernel(tc, xT, w, gate, offs, pos1, pos2, out):
                     )
             w_grouped.append(grouped)
 
-        def tokens(k):
-            a, t0 = chunks[x_calls[k][0]][0:2]
-            n = sum(chunks[i][2] for i in x_calls[k])
-            nc.vector.quantize_mx(
-                out=words[:, first_word(a) + t0 : first_word(a) + t0 + n].bitcast(FP8X4),
-                scales=planes[4 * a : P, t0 : t0 + n],
-                in_=x_grouped[k][:],
-            )
-
-        def gather(dst, window, s, n):
-            nc.vector.tensor_copy(out=dst, in_=window.indirect(offs_sb[:, s // 16 : (s + n) // 16]))
-
         def weights(k):
             u0 = w_chunks[w_calls[k][0]][0]
             n = sum(w_chunks[i][1] for i in w_calls[k])
@@ -137,12 +131,6 @@ def tile_routed_moe_kernel(tc, xT, w, gate, offs, pos1, pos2, out):
                 in_=w_grouped[k][:],
             )
 
-        for a in range(PASSES):
-            for k in range(len(x_calls)):
-                if chunks[x_calls[k][0]][0] == a:
-                    tokens(k)
-            if a < PASSES - 1:
-                gather(early_words[:, a, :], words[:, first_word(a) : first_word(a) + WIDE], 0, SLOTS)
         gather(slot_planes[:], planes[:], 0, SLOTS)
 
         last_window = words[:, 0 : 2 * T]

@@ -33,14 +33,16 @@ def tile_routed_moe_kernel(tc, xT, w, gate, offs, pos1, pos2, out):
         pos2_sb = keep.tile([P, T // 16], U16, name="pos2_sb")
 
         x_view = xT.rearrange("(a p j) n -> a p j n", p=P, j=4)
-        w_view = w.rearrange("e (a p j) n -> p (e a) j n", p=P, j=4)
+        w_view = w.rearrange("e (a p j) n -> p e a j n", p=P, j=4)
 
         x_loads = [(0, 0, 512), (0, 512, 256), (0, 768, 256)]
         x_loads += [(a, t0, 512) for a in (1, 2) for t0 in (0, 512)]
         x_calls = [(0, 0, 256, 256), (0, 256, 256, 0), (0, 512, 256, 64), (0, 768, 256, 192)]
         x_calls += [(1, 0, 512, 0), (1, 512, 512, 160), (2, 0, 512, 0), (2, 512, 512, 0)]
-        w_chunks = [(u0, 4, 1) for u0 in range(0, 20, 4)] + [(20, 2, 0), (22, 2, 0)]
-        w_calls = [[0, 1], [2, 3], [4], [5, 6]]
+        w_chunks = [(u0, 4, 1) for u0 in range(0, 16, 4)] + [(16, 2, 1), (18, 2, 0), (20, 2, 0), (22, 2, 0)]
+        units = [(e, 0) for e in range(E)] + [(e, a) for a in (1, 2) for e in range(4)]
+        units += [(e, a) for e in range(4, E) for a in (1, 2)]
+        w_calls = [[0, 1], [2, 3], [4, 5], [6, 7]]
 
         x_raw = {}
         for i, (a, t0, n) in enumerate(x_loads):
@@ -56,7 +58,9 @@ def tile_routed_moe_kernel(tc, xT, w, gate, offs, pos1, pos2, out):
                 raw = late.tile([P, n, 4, N], F32, align_bytes=64, offset=0, name=f"w_raw{i}")
             else:
                 raw = keep.tile([P, n, 4, N], F32, align_bytes=64, name=f"w_raw{i}")
-            nc.sync.dma_start(out=raw[:], in_=w_view[:, u0 : u0 + n, :, :])
+            e, a = units[u0]
+            src = w_view[:, e : e + n, a, :, :] if n == 4 else w_view[:, e, a : a + n, :, :]
+            nc.sync.dma_start(out=raw[:], in_=src)
             w_raw.append(raw)
         nc.sync.dma_start(pos1_sb[:], pos1)
         nc.sync.dma_start(pos2_sb[:], pos2)
@@ -139,7 +143,7 @@ def tile_routed_moe_kernel(tc, xT, w, gate, offs, pos1, pos2, out):
         gather(late_a[:], last_window, 0, 4 * C)
         weights(1)
         weights(2)
-        late_b = keep.tile([P, 3 * C], U32, align_bytes=64, name="late_b", tag="w_raw4")
+        late_b = keep.tile([P, 3 * C], U32, align_bytes=64, name="late_b", tag="w_raw5")
         gather(late_b[:], last_window, 4 * C, 3 * C)
         weights(3)
         late_c = late.tile([P, C], U32, align_bytes=64, offset=0, name="late_c")
@@ -148,20 +152,18 @@ def tile_routed_moe_kernel(tc, xT, w, gate, offs, pos1, pos2, out):
         last_words += [late_b[:, e * C : (e + 1) * C] for e in range(3)] + [late_c[:]]
 
         accs = [psum.tile([P, C], F32, name=f"acc{e}") for e in range(E)]
-        for e in range(E):
-            for a in range(PASSES):
-                u = e * PASSES + a
-                cols = slice(e * C, (e + 1) * C)
-                rhs = last_words[e] if a == PASSES - 1 else early_words[:, a, cols]
-                nc.tensor.matmul_mx(
-                    out=accs[e][:],
-                    lhsT=w_codes[:, u, :].bitcast(FP8X4),
-                    lhsT_scale=w_scales[:, u, :],
-                    rhs=rhs.bitcast(FP8X4),
-                    rhs_scale=slot_planes[4 * a : P, cols],
-                    start=(a == 0),
-                    stop=(a == PASSES - 1),
-                )
+        for u, (e, a) in enumerate(units):
+            cols = slice(e * C, (e + 1) * C)
+            rhs = last_words[e] if a == PASSES - 1 else early_words[:, a, cols]
+            nc.tensor.matmul_mx(
+                out=accs[e][:],
+                lhsT=w_codes[:, u, :].bitcast(FP8X4),
+                lhsT_scale=w_scales[:, u, :],
+                rhs=rhs.bitcast(FP8X4),
+                rhs_scale=slot_planes[4 * a : P, cols],
+                start=(a == 0),
+                stop=(a == PASSES - 1),
+            )
 
         y = late.tile([P, SLOTS], F32, align_bytes=64, offset=4 * C, name="y")
         for e in range(E):

@@ -26,6 +26,7 @@ def tile_routed_moe_kernel(tc, xT, w, gate, offs, pos1, pos2, out):
     with ExitStack() as ctx:
         keep = ctx.enter_context(tc.tile_pool(name="keep", bufs=1))
         late = ctx.enter_context(tc.tile_pool(name="late", bufs=1))
+        head = ctx.enter_context(tc.tile_pool(name="head", bufs=1))
         psum = ctx.enter_context(tc.psum_pool(name="psum", bufs=1))
 
         offs_sb = keep.tile([P, E * C // 16], U16, name="offs_sb")
@@ -35,11 +36,12 @@ def tile_routed_moe_kernel(tc, xT, w, gate, offs, pos1, pos2, out):
         x_view = xT.rearrange("(a p j) n -> a p j n", p=P, j=4)
         w_view = w.rearrange("e (a p j) n -> p e a j n", p=P, j=4)
 
-        x_loads = [(0, 0, 512), (0, 512, 256), (0, 768, 256)]
+        x_loads = [(0, 0, 512), (0, 512, 384), (0, 896, 128)]
         x_loads += [(a, t0, 512) for a in (1, 2) for t0 in (0, 512)]
-        x_calls = [(0, 0, 256, 256), (0, 256, 256, 0), (0, 512, 256, 64), (0, 768, 256, 192)]
-        x_calls += [(1, 0, 512, 0), (1, 512, 512, 160), (2, 0, 512, 0), (2, 512, 512, 0)]
-        w_chunks = [(u0, 4, 1) for u0 in range(0, 16, 4)] + [(16, 2, 1), (18, 2, 0), (20, 2, 0), (22, 2, 0)]
+        x_calls = [(0, 0, [(256, "v")]), (0, 256, [(256, "s")]), (0, 512, [(256, "v")])]
+        x_calls += [(0, 768, [(128, "s"), (128, "v")])]
+        x_calls += [(1, 0, [(512, "s")]), (1, 512, [(160, "v"), (352, "s")]), (2, 0, [(512, "s"), (512, "s")])]
+        w_chunks = [(0, 4, 0)] + [(u0, 4, 1) for u0 in range(4, 16, 4)] + [(16, 2, 1), (18, 2, 0), (20, 2, 0), (22, 2, 0)]
         units = [(e, 0) for e in range(E)] + [(e, a) for a in (1, 2) for e in range(4)]
         units += [(e, a) for e in range(4, E) for a in (1, 2)]
         w_calls = [[0, 1], [2, 3], [4, 5], [6, 7]]
@@ -48,7 +50,7 @@ def tile_routed_moe_kernel(tc, xT, w, gate, offs, pos1, pos2, out):
         for i, (a, t0, n) in enumerate(x_loads):
             raw = keep.tile([P, 4, n], F32, name=f"x_raw{i}")
             nc.sync.dma_start(out=raw[:], in_=x_view[a, :, :, t0 : t0 + n])
-            for t in range(t0, t0 + n, 128):
+            for t in range(t0, t0 + n, 32):
                 x_raw[(a, t)] = raw[:, :, t - t0 : n]
             if i == 2:
                 nc.sync.dma_start(offs_sb[:], offs)
@@ -74,6 +76,9 @@ def tile_routed_moe_kernel(tc, xT, w, gate, offs, pos1, pos2, out):
         planes = keep.tile([P, WIDE], U8, align_bytes=64, name="planes")
         nc.gpsimd.memset(planes[:, 0:T], 0)
 
+        def plane_row(a):
+            return 4 * ((a + 1) % PASSES)
+
         def first_word(a):
             return (PASSES - 1 - a) * T
 
@@ -85,17 +90,24 @@ def tile_routed_moe_kernel(tc, xT, w, gate, offs, pos1, pos2, out):
         def gather(dst, window, s, n):
             nc.vector.tensor_copy(out=dst, in_=window.indirect(offs_sb[:, s // 16 : (s + n) // 16]))
 
-        for k, (a, t0, n, nv) in enumerate(x_calls):
-            grouped = keep.tile([P, n * 4], BF16, align_bytes=64, name=f"x_grouped{k}", tag=f"x_grouped{k % 2 if a == 0 else k}")
-            dst = grouped[:].rearrange("p (c i j) -> p c j i", i=4, j=4)
-            src = x_raw[(a, t0)][:, :, 0:n].rearrange("p j (c i) -> p c j i", i=4)
-            if nv:
-                nc.vector.tensor_copy(out=dst[:, 0 : nv // 4, :, :], in_=src[:, 0 : nv // 4, :, :])
-            if nv < n:
-                nc.scalar.copy(out=dst[:, nv // 4 : n // 4, :, :], in_=src[:, nv // 4 : n // 4, :, :])
+        for k, (a, t0, shares) in enumerate(x_calls):
+            n = sum(m for m, engine in shares)
+            if k in (1, 2, 3):
+                grouped = head.tile([P, n * 4], BF16, align_bytes=64, offset=(1024, 2048, 0)[k - 1], name=f"x_grouped{k}")
+            else:
+                grouped = keep.tile([P, n * 4], BF16, align_bytes=64, name=f"x_grouped{k}")
+            t1 = 0
+            for m, engine in shares:
+                dst = grouped[:, 4 * t1 : 4 * (t1 + m)].rearrange("p (c i j) -> p c j i", i=4, j=4)
+                src = x_raw[(a, t0 + t1)][:, :, 0:m].rearrange("p j (c i) -> p c j i", i=4)
+                if engine == "v":
+                    nc.vector.tensor_copy(out=dst, in_=src)
+                else:
+                    nc.scalar.copy(out=dst, in_=src)
+                t1 += m
             nc.vector.quantize_mx(
                 out=words[:, first_word(a) + t0 : first_word(a) + t0 + n].bitcast(FP8X4),
-                scales=planes[4 * a : P, t0 : t0 + n],
+                scales=planes[plane_row(a) : P, t0 : t0 + n],
                 in_=grouped[:],
             )
             if t0 + n == T and a < PASSES - 1:
@@ -160,7 +172,7 @@ def tile_routed_moe_kernel(tc, xT, w, gate, offs, pos1, pos2, out):
                 lhsT=w_codes[:, u, :].bitcast(FP8X4),
                 lhsT_scale=w_scales[:, u, :],
                 rhs=rhs.bitcast(FP8X4),
-                rhs_scale=slot_planes[4 * a : P, cols],
+                rhs_scale=slot_planes[plane_row(a) : P, cols],
                 start=(a == 0),
                 stop=(a == PASSES - 1),
             )

@@ -37,11 +37,12 @@ def tile_routed_moe_kernel(tc, xT, w, gate, offs, pos1, pos2, out):
         w_view = w.rearrange("e (a p j) n -> p e a j n", p=P, j=4)
 
         x_loads = [(0, 0, 512), (0, 512, 384), (0, 896, 128)]
-        x_loads += [(a, t0, 512) for a in (1, 2) for t0 in (0, 512)]
+        x_loads += [(1, 0, 384), (1, 384, 320), (1, 704, 320), (2, 0, 512), (2, 512, 512)]
         x_calls = [(0, 0, [(256, "v")]), (0, 256, [(256, "s")]), (0, 512, [(256, "v")])]
         x_calls += [(0, 768, [(128, "s"), (128, "v")])]
-        x_calls += [(1, 0, [(512, "s")]), (1, 512, [(160, "v"), (352, "s")]), (2, 0, [(512, "s"), (512, "s")])]
-        w_chunks = [(0, 4, 0)] + [(u0, 4, 1) for u0 in range(4, 16, 4)] + [(16, 2, 1), (18, 2, 0), (20, 2, 0), (22, 2, 0)]
+        x_calls += [(1, 0, [(384, "s"), (128, "s")]), (1, 512, [(192, "s"), (64, "s")]), (1, 768, [(256, "s")])]
+        x_calls += [(2, 0, [(512, "s")]), (2, 512, [(512, "s")])]
+        w_chunks = [(0, 4, 0)] + [(u0, 4, 1) for u0 in range(4, 16, 4)] + [(16, 2, 1), (18, 2, 0), (20, 2, 0), (22, 2, 1)]
         units = [(e, 0) for e in range(E)] + [(e, a) for a in (1, 2) for e in range(4)]
         units += [(e, a) for e in range(4, E) for a in (1, 2)]
         w_calls = [[0, 1], [2, 3], [4, 5], [6, 7]]

@@ -128,10 +128,8 @@ def tile_routed_moe_kernel(tc, xT, w, gate, offs, pos1, pos2, out):
                 )
                 for u in range(ns, n):
                     nc.gpsimd.tensor_scalar(
-                        out=grouped[:, c0 + u * 4 * N : c0 + (u + 1) * 4 * N].rearrange(
-                            "p (c i j) -> p c j i", i=4, j=4
-                        ),
-                        in0=w_raw[i][:, u, :, :].rearrange("p j (c i) -> p c j i", i=4),
+                        out=grouped[:, c0 + u * 4 * N : c0 + (u + 1) * 4 * N].rearrange("p (c j) -> p c j", j=4),
+                        in0=w_raw[i][:, u, :, :].rearrange("p j c -> p c j"),
                         scalar1=1.0,
                         scalar2=0.0,
                         op0=MULT,

@@ -37,11 +37,11 @@ def tile_routed_moe_kernel(tc, xT, w, gate, offs, pos1, pos2, out):
         w_view = w.rearrange("e (a p j) n -> p e a j n", p=P, j=4)
 
         x_loads = [(0, 0, 512), (0, 512, 384), (0, 896, 128)]
-        x_loads += [(1, 0, 384), (1, 384, 320), (1, 704, 320), (2, 0, 512), (2, 512, 512)]
+        x_loads += [(1, 0, 512), (1, 512, 512), (2, 0, 512), (2, 512, 512)]
         x_calls = [(0, 0, [(256, "v")]), (0, 256, [(256, "s")]), (0, 512, [(256, "v")])]
         x_calls += [(0, 768, [(128, "s"), (128, "v")])]
-        x_calls += [(1, 0, [(384, "s"), (128, "s")]), (1, 512, [(192, "s"), (64, "s")]), (1, 768, [(256, "s")])]
-        x_calls += [(2, 0, [(512, "s")]), (2, 512, [(512, "s")])]
+        x_calls += [(1, 0, [(512, "s")]), (1, 512, [(320, "s"), (192, "g")])]
+        x_calls += [(2, 0, [(512, "s")]), (2, 512, [(320, "s"), (192, "g")])]
         w_chunks = [(0, 4, 0)] + [(u0, 4, 1) for u0 in range(4, 16, 4)] + [(16, 2, 1), (18, 2, 0), (20, 2, 0), (22, 2, 1)]
         units = [(e, 0) for e in range(E)] + [(e, a) for a in (1, 2) for e in range(4)]
         units += [(e, a) for e in range(4, E) for a in (1, 2)]
@@ -103,8 +103,13 @@ def tile_routed_moe_kernel(tc, xT, w, gate, offs, pos1, pos2, out):
                 src = x_raw[(a, t0 + t1)][:, :, 0:m].rearrange("p j (c i) -> p c j i", i=4)
                 if engine == "v":
                     nc.vector.tensor_copy(out=dst, in_=src)
-                else:
+                elif engine == "s":
                     nc.scalar.copy(out=dst, in_=src)
+                else:
+                    nc.gpsimd.tensor_copy(
+                        out=grouped[:, 4 * t1 : 4 * (t1 + m)].rearrange("p (c j) -> p c j", j=4),
+                        in_=x_raw[(a, t0 + t1)][:, :, 0:m].rearrange("p j c -> p c j"),
+                    )
                 t1 += m
             nc.vector.quantize_mx(
                 out=words[:, first_word(a) + t0 : first_word(a) + t0 + n].bitcast(FP8X4),

@@ -1,6 +1,7 @@
 from contextlib import ExitStack
 
 import concourse.mybir as mybir
+from concourse.masks import make_identity
 
 K, T, E, C, N = 1536, 1024, 8, 256, 128
 FLOPS = 2 * K * N * E * C
@@ -37,11 +38,11 @@ def tile_routed_moe_kernel(tc, xT, w, gate, offs, pos1, pos2, out):
         w_view = w.rearrange("e (a p j) n -> p e a j n", p=P, j=4)
 
         x_loads = [(0, 0, 512), (0, 512, 384), (0, 896, 128)]
-        x_loads += [(1, 0, 512), (1, 512, 512), (2, 0, 512), (2, 512, 512)]
+        x_loads += [(1, 0, 512), (1, 512, 512), (2, 0, 1024)]
         x_calls = [(0, 0, [(256, "v")]), (0, 256, [(256, "s")]), (0, 512, [(256, "v")])]
         x_calls += [(0, 768, [(128, "s"), (128, "v")])]
         x_calls += [(1, 0, [(512, "s")]), (1, 512, [(320, "s"), (192, "g")])]
-        x_calls += [(2, 0, [(512, "s")]), (2, 512, [(320, "s"), (192, "g")])]
+        x_calls += [(2, 0, [(512, "s")]), (2, 512, [(160, "s"), (352, "g")])]
         w_chunks = [(0, 4, 0)] + [(u0, 4, 1) for u0 in range(4, 16, 4)] + [(16, 2, 1), (18, 2, 0), (20, 2, 0), (22, 2, 1)]
         units = [(e, 0) for e in range(E)] + [(e, a) for a in (1, 2) for e in range(4)]
         units += [(e, a) for e in range(4, E) for a in (1, 2)]
@@ -76,6 +77,9 @@ def tile_routed_moe_kernel(tc, xT, w, gate, offs, pos1, pos2, out):
         words = keep.tile([P, (PASSES - 1) * T + WIDE], U32, align_bytes=64, name="words")
         planes = keep.tile([P, WIDE], U8, align_bytes=64, name="planes")
         nc.gpsimd.memset(planes[:, 0:T], 0)
+
+        identity = keep.tile([P, P], F32, name="identity")
+        make_identity(nc, identity[:])
 
         def plane_row(a):
             return 4 * ((a + 1) % PASSES)
@@ -185,13 +189,33 @@ def tile_routed_moe_kernel(tc, xT, w, gate, offs, pos1, pos2, out):
         for e in range(E):
             nc.scalar.copy(out=y[:, e * C : (e + 1) * C], in_=accs[e][:])
 
-        for i, (t0, n) in enumerate([(0, 768), (768, 256)]):
-            first = keep.tile([P, n], F32, name=f"first{i}")
-            second = keep.tile([P, n], F32, name=f"second{i}")
+        parts = [(0, 384), (384, 384), (768, 256)]
+        products = []
+        for i, (t0, n) in enumerate(parts):
+            products.append([keep.tile([P, n], F32, name=f"product{i}{r}") for r in range(2)])
+
+        def product(i, r):
+            t0, n = parts[i]
+            pos_sb = (pos1_sb, pos2_sb)[r]
+            nc.vector.tensor_tensor(
+                products[i][r][:], y[:].indirect(pos_sb[:, t0 // 16 : (t0 + n) // 16]), gates[r][:, t0 : t0 + n], MULT
+            )
+
+        def finish(i):
+            t0, n = parts[i]
             total = keep.tile([P, n], F32, name=f"total{i}")
-            for dst, pos_sb, g in ((first, pos1_sb, gates[0]), (second, pos2_sb, gates[1])):
-                nc.vector.tensor_tensor(
-                    dst[:], y[:].indirect(pos_sb[:, t0 // 16 : (t0 + n) // 16]), g[:, t0 : t0 + n], MULT
-                )
-            nc.vector.tensor_tensor(total[:], first[:], second[:], ADD)
+            if i < 1:
+                bank = psum.tile([P, n], F32, name=f"bank{i}", tag=f"acc{i}")
+                for r in range(2):
+                    nc.tensor.matmul(bank[:], identity[:], products[i][r][:], start=(r == 0), stop=(r == 1))
+                nc.scalar.copy(out=total[:], in_=bank[:])
+            else:
+                nc.vector.tensor_tensor(total[:], products[i][0][:], products[i][1][:], ADD)
             nc.sync.dma_start(out=out[:, t0 : t0 + n], in_=total[:])
+
+        for i in range(len(parts)):
+            product(i, 0)
+            if i > 0:
+                finish(i - 1)
+            product(i, 1)
+        finish(len(parts) - 1)

@@ -1,7 +1,6 @@
 from contextlib import ExitStack
 
 import concourse.mybir as mybir
-from concourse.masks import make_identity
 
 K, T, E, C, N = 1536, 1024, 8, 256, 128
 FLOPS = 2 * K * N * E * C
@@ -14,6 +13,7 @@ U8 = mybir.dt.uint8
 FP8X4 = mybir.dt.float8_e4m3fn_x4
 MULT = mybir.AluOpType.mult
 ADD = mybir.AluOpType.add
+COPY = mybir.ActivationFunctionType.Copy
 
 P = 128
 PASSES = K // 512
@@ -77,9 +77,6 @@ def tile_routed_moe_kernel(tc, xT, w, gate, offs, pos1, pos2, out):
         words = keep.tile([P, (PASSES - 1) * T + WIDE], U32, align_bytes=64, name="words")
         planes = keep.tile([P, WIDE], U8, align_bytes=64, name="planes")
         nc.gpsimd.memset(planes[:, 0:T], 0)
-
-        identity = keep.tile([P, P], F32, name="identity")
-        make_identity(nc, identity[:])
 
         def plane_row(a):
             return 4 * ((a + 1) % PASSES)
@@ -189,33 +186,40 @@ def tile_routed_moe_kernel(tc, xT, w, gate, offs, pos1, pos2, out):
         for e in range(E):
             nc.scalar.copy(out=y[:, e * C : (e + 1) * C], in_=accs[e][:])
 
-        parts = [(0, 384), (384, 384), (768, 256)]
-        products = []
-        for i, (t0, n) in enumerate(parts):
-            products.append([keep.tile([P, n], F32, name=f"product{i}{r}") for r in range(2)])
+        parts = [(0, 384, (0,)), (384, 384, ()), (768, 256, (0,))]
+        lists = (pos1_sb, pos2_sb)
+        fetched = {}
+        products = {}
+
+        def window(i, r):
+            t0, n, fused = parts[i]
+            return y[:].indirect(lists[r][:, t0 // 16 : (t0 + n) // 16])
+
+        def fetch(i, r):
+            fetched[(i, r)] = keep.tile([P, parts[i][1]], F32, name=f"fetched{i}{r}")
+            nc.scalar.activation(fetched[(i, r)][:], window(i, r), COPY)
 
         def product(i, r):
-            t0, n = parts[i]
-            pos_sb = (pos1_sb, pos2_sb)[r]
-            nc.vector.tensor_tensor(
-                products[i][r][:], y[:].indirect(pos_sb[:, t0 // 16 : (t0 + n) // 16]), gates[r][:, t0 : t0 + n], MULT
-            )
+            t0, n, fused = parts[i]
+            products[(i, r)] = keep.tile([P, n], F32, name=f"product{i}{r}")
+            src = window(i, r) if r in fused else fetched[(i, r)][:]
+            nc.vector.tensor_tensor(products[(i, r)][:], src, gates[r][:, t0 : t0 + n], MULT)
 
         def finish(i):
-            t0, n = parts[i]
+            t0, n, fused = parts[i]
             total = keep.tile([P, n], F32, name=f"total{i}")
-            if i < 1:
-                bank = psum.tile([P, n], F32, name=f"bank{i}", tag=f"acc{i}")
-                for r in range(2):
-                    nc.tensor.matmul(bank[:], identity[:], products[i][r][:], start=(r == 0), stop=(r == 1))
-                nc.scalar.copy(out=total[:], in_=bank[:])
-            else:
-                nc.vector.tensor_tensor(total[:], products[i][0][:], products[i][1][:], ADD)
+            nc.vector.tensor_tensor(total[:], products[(i, 0)][:], products[(i, 1)][:], ADD)
             nc.sync.dma_start(out=out[:, t0 : t0 + n], in_=total[:])
 
         for i in range(len(parts)):
-            product(i, 0)
-            if i > 0:
-                finish(i - 1)
-            product(i, 1)
-        finish(len(parts) - 1)
+            for r in range(2):
+                if r not in parts[i][2]:
+                    fetch(i, r)
+        for i in range(len(parts)):
+            for r in parts[i][2]:
+                product(i, r)
+        for i in range(len(parts)):
+            for r in range(2):
+                if r not in parts[i][2]:
+                    product(i, r)
+            finish(i)

@@ -68,11 +68,9 @@ def tile_routed_moe_kernel(tc, xT, w, gate, offs, pos1, pos2, out):
             w_raw.append(raw)
         nc.sync.dma_start(pos1_sb[:], pos1)
         nc.sync.dma_start(pos2_sb[:], pos2)
-        gates = []
+        gates = keep.tile([P, 2, T], F32, name="gates")
         for r in range(2):
-            g = keep.tile([P, T], F32, name=f"gate{r}")
-            nc.sync.dma_start(out=g[:], in_=gate[r, :, :])
-            gates.append(g)
+            nc.sync.dma_start(out=gates[:, r, :], in_=gate[r, :, :])
 
         words = keep.tile([P, (PASSES - 1) * T + WIDE], U32, align_bytes=64, name="words")
         planes = keep.tile([P, WIDE], U8, align_bytes=64, name="planes")
@@ -186,40 +184,32 @@ def tile_routed_moe_kernel(tc, xT, w, gate, offs, pos1, pos2, out):
         for e in range(E):
             nc.scalar.copy(out=y[:, e * C : (e + 1) * C], in_=accs[e][:])
 
-        parts = [(0, 384, (0,)), (384, 384, ()), (768, 256, (0,))]
+        both = 256
+        parts = [(256, 384), (640, 256), (896, 128)]
         lists = (pos1_sb, pos2_sb)
-        fetched = {}
-        products = {}
 
-        def window(i, r):
-            t0, n, fused = parts[i]
+        def window(r, t0, n):
             return y[:].indirect(lists[r][:, t0 // 16 : (t0 + n) // 16])
 
-        def fetch(i, r):
-            fetched[(i, r)] = keep.tile([P, parts[i][1]], F32, name=f"fetched{i}{r}")
-            nc.scalar.activation(fetched[(i, r)][:], window(i, r), COPY)
+        fetched = keep.tile([P, 2, both], F32, name="fetched")
+        for r in range(2):
+            nc.scalar.activation(fetched[:, r, :], window(r, 0, both), COPY)
+        second = []
+        for i, (t0, n) in enumerate(parts):
+            second.append(keep.tile([P, n], F32, name=f"second{i}"))
+            nc.scalar.activation(second[i][:], window(1, t0, n), COPY)
 
-        def product(i, r):
-            t0, n, fused = parts[i]
-            products[(i, r)] = keep.tile([P, n], F32, name=f"product{i}{r}")
-            src = window(i, r) if r in fused else fetched[(i, r)][:]
-            nc.vector.tensor_tensor(products[(i, r)][:], src, gates[r][:, t0 : t0 + n], MULT)
-
-        def finish(i):
-            t0, n, fused = parts[i]
-            total = keep.tile([P, n], F32, name=f"total{i}")
-            nc.vector.tensor_tensor(total[:], products[(i, 0)][:], products[(i, 1)][:], ADD)
+        def finish(name, t0, n, p0, p1):
+            total = keep.tile([P, n], F32, name=name)
+            nc.vector.tensor_tensor(total[:], p0, p1, ADD)
             nc.sync.dma_start(out=out[:, t0 : t0 + n], in_=total[:])
 
-        for i in range(len(parts)):
-            for r in range(2):
-                if r not in parts[i][2]:
-                    fetch(i, r)
-        for i in range(len(parts)):
-            for r in parts[i][2]:
-                product(i, r)
-        for i in range(len(parts)):
-            for r in range(2):
-                if r not in parts[i][2]:
-                    product(i, r)
-            finish(i)
+        first = keep.tile([P, T - both], F32, name="first")
+        nc.vector.tensor_tensor(first[:], window(0, both, T - both), gates[:, 0, both:T], MULT)
+        pair = keep.tile([P, 2, both], F32, name="pair")
+        nc.vector.tensor_tensor(pair[:], fetched[:], gates[:, :, 0:both], MULT)
+        finish("total", 0, both, pair[:, 0, :], pair[:, 1, :])
+        for i, (t0, n) in enumerate(parts):
+            product = keep.tile([P, n], F32, name=f"product{i}")
+            nc.vector.tensor_tensor(product[:], second[i][:], gates[:, 1, t0 : t0 + n], MULT)
+            finish(f"total{i}", t0, n, first[:, t0 - both : t0 - both + n], product[:])

@@ -184,32 +184,16 @@ def tile_routed_moe_kernel(tc, xT, w, gate, offs, pos1, pos2, out):
         for e in range(E):
             nc.scalar.copy(out=y[:, e * C : (e + 1) * C], in_=accs[e][:])
 
-        both = 256
-        parts = [(256, 384), (640, 256), (896, 128)]
-        lists = (pos1_sb, pos2_sb)
-
-        def window(r, t0, n):
-            return y[:].indirect(lists[r][:, t0 // 16 : (t0 + n) // 16])
-
-        fetched = keep.tile([P, 2, both], F32, name="fetched")
-        for r in range(2):
-            nc.scalar.activation(fetched[:, r, :], window(r, 0, both), COPY)
+        parts = [(0, 512), (512, 320), (832, 192)]
         second = []
         for i, (t0, n) in enumerate(parts):
             second.append(keep.tile([P, n], F32, name=f"second{i}"))
-            nc.scalar.activation(second[i][:], window(1, t0, n), COPY)
-
-        def finish(name, t0, n, p0, p1):
-            total = keep.tile([P, n], F32, name=name)
-            nc.vector.tensor_tensor(total[:], p0, p1, ADD)
-            nc.sync.dma_start(out=out[:, t0 : t0 + n], in_=total[:])
-
-        first = keep.tile([P, T - both], F32, name="first")
-        nc.vector.tensor_tensor(first[:], window(0, both, T - both), gates[:, 0, both:T], MULT)
-        pair = keep.tile([P, 2, both], F32, name="pair")
-        nc.vector.tensor_tensor(pair[:], fetched[:], gates[:, :, 0:both], MULT)
-        finish("total", 0, both, pair[:, 0, :], pair[:, 1, :])
+            nc.scalar.activation(second[i][:], y[:].indirect(pos2_sb[:, t0 // 16 : (t0 + n) // 16]), COPY)
+        first = keep.tile([P, T], F32, name="first")
+        nc.vector.tensor_tensor(first[:], y[:].indirect(pos1_sb[:]), gates[:, 0, :], MULT)
         for i, (t0, n) in enumerate(parts):
             product = keep.tile([P, n], F32, name=f"product{i}")
             nc.vector.tensor_tensor(product[:], second[i][:], gates[:, 1, t0 : t0 + n], MULT)
-            finish(f"total{i}", t0, n, first[:, t0 - both : t0 - both + n], product[:])
+            total = keep.tile([P, n], F32, name=f"total{i}")
+            nc.vector.tensor_tensor(total[:], first[:, t0 : t0 + n], product[:], ADD)
+            nc.sync.dma_start(out=out[:, t0 : t0 + n], in_=total[:])

@@ -38,11 +38,11 @@ def tile_routed_moe_kernel(tc, xT, w, gate, offs, pos1, pos2, out):
         w_view = w.rearrange("e (a p j) n -> p e a j n", p=P, j=4)
 
         x_loads = [(0, 0, 512), (0, 512, 384), (0, 896, 128)]
-        x_loads += [(1, 0, 512), (1, 512, 512), (2, 0, 1024)]
-        x_calls = [(0, 0, [(256, "v")]), (0, 256, [(256, "s")]), (0, 512, [(256, "v")])]
-        x_calls += [(0, 768, [(128, "s"), (128, "v")])]
-        x_calls += [(1, 0, [(512, "s")]), (1, 512, [(320, "s"), (192, "g")])]
-        x_calls += [(2, 0, [(512, "s")]), (2, 512, [(160, "s"), (352, "g")])]
+        x_loads += [(1, 0, 512), (1, 512, 512), (2, 0, 512), (2, 512, 512)]
+        x_calls = [(0, 0, [(256, "v")], [256]), (0, 256, [(256, "s")], [256])]
+        x_calls += [(0, 512, [(320, "v"), (64, "s"), (128, "s")], [256, 256])]
+        x_calls += [(1, 0, [(512, "s")], [512]), (1, 512, [(320, "s"), (192, "g")], [512])]
+        x_calls += [(2, 0, [(512, "s"), (384, "s"), (128, "g")], [1024])]
         w_chunks = [(0, 4, 0)] + [(u0, 4, 1) for u0 in range(4, 16, 4)] + [(16, 2, 1), (18, 2, 0), (20, 2, 0), (22, 2, 1)]
         units = [(e, 0) for e in range(E)] + [(e, a) for a in (1, 2) for e in range(4)]
         units += [(e, a) for e in range(4, E) for a in (1, 2)]
@@ -90,10 +90,10 @@ def tile_routed_moe_kernel(tc, xT, w, gate, offs, pos1, pos2, out):
         def gather(dst, window, s, n):
             nc.vector.tensor_copy(out=dst, in_=window.indirect(offs_sb[:, s // 16 : (s + n) // 16]))
 
-        for k, (a, t0, shares) in enumerate(x_calls):
-            n = sum(m for m, engine in shares)
-            if k in (1, 2, 3):
-                grouped = head.tile([P, n * 4], BF16, align_bytes=64, offset=(1024, 2048, 0)[k - 1], name=f"x_grouped{k}")
+        for k, (a, t0, shares, widths) in enumerate(x_calls):
+            n = sum(widths)
+            if k in (1, 2):
+                grouped = head.tile([P, n * 4], BF16, align_bytes=64, name=f"x_grouped{k}", tag="head")
             else:
                 grouped = keep.tile([P, n * 4], BF16, align_bytes=64, name=f"x_grouped{k}")
             t1 = 0
@@ -110,11 +110,14 @@ def tile_routed_moe_kernel(tc, xT, w, gate, offs, pos1, pos2, out):
                         in_=x_raw[(a, t0 + t1)][:, :, 0:m].rearrange("p j c -> p c j"),
                     )
                 t1 += m
-            nc.vector.quantize_mx(
-                out=words[:, first_word(a) + t0 : first_word(a) + t0 + n].bitcast(FP8X4),
-                scales=planes[plane_row(a) : P, t0 : t0 + n],
-                in_=grouped[:],
-            )
+            t1 = 0
+            for m in widths:
+                nc.vector.quantize_mx(
+                    out=words[:, first_word(a) + t0 + t1 : first_word(a) + t0 + t1 + m].bitcast(FP8X4),
+                    scales=planes[plane_row(a) : P, t0 + t1 : t0 + t1 + m],
+                    in_=grouped[:, 4 * t1 : 4 * (t1 + m)],
+                )
+                t1 += m
             if t0 + n == T and a < PASSES - 1:
                 gather(early_words[:, a, :], words[:, first_word(a) : first_word(a) + WIDE], 0, SLOTS)
         w_grouped = []

@@ -38,10 +38,10 @@ def tile_routed_moe_kernel(tc, xT, w, gate, offs, pos1, pos2, out):
         w_view = w.rearrange("e (a p j) n -> p e a j n", p=P, j=4)
 
         x_loads = [(0, 0, 512), (0, 512, 384), (0, 896, 128)]
-        x_loads += [(1, 0, 512), (1, 512, 512), (2, 0, 512), (2, 512, 512)]
+        x_loads += [(1, 0, 640), (1, 640, 384), (2, 0, 512), (2, 512, 512)]
         x_calls = [(0, 0, [(256, "v")], [256]), (0, 256, [(256, "s")], [256])]
         x_calls += [(0, 512, [(320, "v"), (64, "s"), (128, "s")], [256, 256])]
-        x_calls += [(1, 0, [(512, "s")], [512]), (1, 512, [(320, "s"), (192, "g")], [512])]
+        x_calls += [(1, 0, [(384, "s"), (256, "g"), (256, "s"), (128, "g")], [512, 512])]
         x_calls += [(2, 0, [(512, "s"), (384, "s"), (128, "g")], [1024])]
         w_chunks = [(0, 4, 0)] + [(u0, 4, 1) for u0 in range(4, 16, 4)] + [(16, 2, 1), (18, 2, 0), (20, 2, 0), (22, 2, 1)]
         units = [(e, 0) for e in range(E)] + [(e, a) for a in (1, 2) for e in range(4)]

@@ -38,11 +38,11 @@ def tile_routed_moe_kernel(tc, xT, w, gate, offs, pos1, pos2, out):
         w_view = w.rearrange("e (a p j) n -> p e a j n", p=P, j=4)
 
         x_loads = [(0, 0, 512), (0, 512, 384), (0, 896, 128)]
-        x_loads += [(1, 0, 640), (1, 640, 384), (2, 0, 512), (2, 512, 512)]
+        x_loads += [(1, 0, 640), (1, 640, 384), (2, 0, 1024)]
         x_calls = [(0, 0, [(256, "v")], [256]), (0, 256, [(256, "s")], [256])]
         x_calls += [(0, 512, [(320, "v"), (64, "s"), (128, "s")], [256, 256])]
         x_calls += [(1, 0, [(384, "s"), (256, "g"), (256, "s"), (128, "g")], [512, 512])]
-        x_calls += [(2, 0, [(512, "s"), (384, "s"), (128, "g")], [1024])]
+        x_calls += [(2, 0, [(512, "s"), (128, "s"), (384, "g")], [512, 512])]
         w_chunks = [(0, 4, 0)] + [(u0, 4, 1) for u0 in range(4, 16, 4)] + [(16, 2, 1), (18, 2, 0), (20, 2, 0), (22, 2, 1)]
         units = [(e, 0) for e in range(E)] + [(e, a) for a in (1, 2) for e in range(4)]
         units += [(e, a) for e in range(4, E) for a in (1, 2)]

@@ -43,7 +43,7 @@ def tile_routed_moe_kernel(tc, xT, w, gate, offs, pos1, pos2, out):
         x_calls += [(0, 512, [(320, "v"), (64, "s"), (128, "s")], [256, 256])]
         x_calls += [(1, 0, [(384, "s"), (256, "g"), (256, "s"), (128, "g")], [512, 512])]
         x_calls += [(2, 0, [(512, "s"), (128, "s"), (384, "g")], [512, 512])]
-        w_chunks = [(0, 4, 0)] + [(u0, 4, 1) for u0 in range(4, 16, 4)] + [(16, 2, 1), (18, 2, 0), (20, 2, 0), (22, 2, 1)]
+        w_chunks = [(0, 4, 0)] + [(u0, 4, 1) for u0 in range(4, 16, 4)] + [(16, 2, 0), (18, 2, 0), (20, 2, 0), (22, 2, 1)]
         units = [(e, 0) for e in range(E)] + [(e, a) for a in (1, 2) for e in range(4)]
         units += [(e, a) for e in range(4, E) for a in (1, 2)]
         w_calls = [[0, 1], [2, 3], [4, 5], [6, 7]]

@@ -169,23 +169,28 @@ def tile_routed_moe_kernel(tc, xT, w, gate, offs, pos1, pos2, out):
         last_words = [late_a[:, e * C : (e + 1) * C] for e in range(4)]
         last_words += [late_b[:, e * C : (e + 1) * C] for e in range(3)] + [late_c[:]]
 
-        accs = [psum.tile([P, C], F32, name=f"acc{e}") for e in range(E)]
-        for u, (e, a) in enumerate(units):
+        pair = psum.tile([P, 2 * C], F32, name="pair")
+        accs = [pair[:, (e - 4) * C : (e - 3) * C] if e in (4, 5) else psum.tile([P, C], F32, name=f"acc{e}")[:] for e in range(E)]
+        order = units[:16] + [(e, a) for a in (1, 2) for e in (4, 5)] + units[20:]
+        for e, a in order:
+            u = units.index((e, a))
             cols = slice(e * C, (e + 1) * C)
             rhs = last_words[e] if a == PASSES - 1 else early_words[:, a, cols]
             nc.tensor.matmul_mx(
-                out=accs[e][:],
+                out=accs[e],
                 lhsT=w_codes[:, u, :].bitcast(FP8X4),
                 lhsT_scale=w_scales[:, u, :],
                 rhs=rhs.bitcast(FP8X4),
                 rhs_scale=slot_planes[plane_row(a) : P, cols],
-                start=(a == 0),
-                stop=(a == PASSES - 1),
+                start=(a == 0 and e != 5),
+                stop=(a == PASSES - 1 and e != 4),
             )
 
         y = late.tile([P, SLOTS], F32, align_bytes=64, offset=4 * C, name="y")
+        nc.vector.tensor_copy(out=y[:, 4 * C : 6 * C], in_=pair[:])
         for e in range(E):
-            nc.scalar.copy(out=y[:, e * C : (e + 1) * C], in_=accs[e][:])
+            if e not in (4, 5):
+                nc.scalar.copy(out=y[:, e * C : (e + 1) * C], in_=accs[e])
 
         parts = [(0, 512), (512, 320), (832, 192)]
         second = []

@@ -192,16 +192,28 @@ def tile_routed_moe_kernel(tc, xT, w, gate, offs, pos1, pos2, out):
             if e not in (4, 5):
                 nc.scalar.copy(out=y[:, e * C : (e + 1) * C], in_=accs[e])
 
-        parts = [(0, 512), (512, 320), (832, 192)]
+        parts = [(0, 512), (512, 256), (768, 256)]
         second = []
         for i, (t0, n) in enumerate(parts):
             second.append(keep.tile([P, n], F32, name=f"second{i}"))
             nc.scalar.activation(second[i][:], y[:].indirect(pos2_sb[:, t0 // 16 : (t0 + n) // 16]), COPY)
         first = keep.tile([P, T], F32, name="first")
         nc.vector.tensor_tensor(first[:], y[:].indirect(pos1_sb[:]), gates[:, 0, :], MULT)
-        for i, (t0, n) in enumerate(parts):
-            product = keep.tile([P, n], F32, name=f"product{i}")
-            nc.vector.tensor_tensor(product[:], second[i][:], gates[:, 1, t0 : t0 + n], MULT)
+        products = []
+
+        def multiply(i):
+            t0, n = parts[i]
+            products.append(keep.tile([P, n], F32, name=f"product{i}"))
+            nc.vector.tensor_tensor(products[i][:], second[i][:], gates[:, 1, t0 : t0 + n], MULT)
+
+        def add_and_store(i):
+            t0, n = parts[i]
             total = keep.tile([P, n], F32, name=f"total{i}")
-            nc.vector.tensor_tensor(total[:], first[:, t0 : t0 + n], product[:], ADD)
+            nc.vector.tensor_tensor(total[:], first[:, t0 : t0 + n], products[i][:], ADD)
             nc.sync.dma_start(out=out[:, t0 : t0 + n], in_=total[:])
+
+        multiply(0)
+        for i in range(1, len(parts)):
+            multiply(i)
+            add_and_store(i - 1)
+        add_and_store(len(parts) - 1)

@@ -192,28 +192,39 @@ def tile_routed_moe_kernel(tc, xT, w, gate, offs, pos1, pos2, out):
             if e not in (4, 5):
                 nc.scalar.copy(out=y[:, e * C : (e + 1) * C], in_=accs[e])
 
-        parts = [(0, 512), (512, 256), (768, 256)]
-        second = []
-        for i, (t0, n) in enumerate(parts):
-            second.append(keep.tile([P, n], F32, name=f"second{i}"))
-            nc.scalar.activation(second[i][:], y[:].indirect(pos2_sb[:, t0 // 16 : (t0 + n) // 16]), COPY)
-        first = keep.tile([P, T], F32, name="first")
-        nc.vector.tensor_tensor(first[:], y[:].indirect(pos1_sb[:]), gates[:, 0, :], MULT)
-        products = []
+        both = T - 128
+        fetched = keep.tile([P, T + (T - both)], F32, name="fetched")
+        for t0, t1 in ((0, 640), (640, both)):
+            nc.scalar.activation(fetched[:, t0:t1], y[:].indirect(pos2_sb[:, t0 // 16 : t1 // 16]), COPY)
+        nc.scalar.activation(fetched[:, both:T], y[:].indirect(pos1_sb[:, both // 16 :]), COPY)
+        nc.scalar.activation(fetched[:, T:], y[:].indirect(pos2_sb[:, both // 16 :]), COPY)
+        first = keep.tile([P, both], F32, name="first")
+        product = keep.tile([P, T + (T - both)], F32, name="product")
+        total = keep.tile([P, T], F32, name="total")
 
-        def multiply(i):
-            t0, n = parts[i]
-            products.append(keep.tile([P, n], F32, name=f"product{i}"))
-            nc.vector.tensor_tensor(products[i][:], second[i][:], gates[:, 1, t0 : t0 + n], MULT)
+        def multiply(t0, t1):
+            nc.vector.tensor_tensor(product[:, t0:t1], fetched[:, t0:t1], gates[:, 1, t0:t1], MULT)
 
-        def add_and_store(i):
-            t0, n = parts[i]
-            total = keep.tile([P, n], F32, name=f"total{i}")
-            nc.vector.tensor_tensor(total[:], first[:, t0 : t0 + n], products[i][:], ADD)
-            nc.sync.dma_start(out=out[:, t0 : t0 + n], in_=total[:])
+        def add(t0, t1):
+            nc.vector.tensor_tensor(total[:, t0:t1], first[:, t0:t1], product[:, t0:t1], ADD)
 
-        multiply(0)
-        for i in range(1, len(parts)):
-            multiply(i)
-            add_and_store(i - 1)
-        add_and_store(len(parts) - 1)
+        def store(t0, t1):
+            nc.sync.dma_start(out=out[:, t0:t1], in_=total[:, t0:t1])
+
+        nc.vector.tensor_tensor(first[:], y[:].indirect(pos1_sb[:, 0 : both // 16]), gates[:, 0, 0:both], MULT)
+        multiply(0, 384)
+        multiply(384, 640)
+        add(0, 384)
+        store(0, 384)
+        multiply(640, both)
+        add(384, 640)
+        add(640, both)
+        store(384, both)
+        nc.vector.tensor_tensor(
+            product[:, both:].rearrange("p (r t) -> p r t", r=2),
+            fetched[:, both:].rearrange("p (r t) -> p r t", r=2),
+            gates[:, :, both:],
+            MULT,
+        )
+        nc.vector.tensor_tensor(total[:, both:], product[:, both:T], product[:, T:], ADD)
+        store(both, T)

@@ -193,38 +193,25 @@ def tile_routed_moe_kernel(tc, xT, w, gate, offs, pos1, pos2, out):
                 nc.scalar.copy(out=y[:, e * C : (e + 1) * C], in_=accs[e])
 
         both = T - 128
-        fetched = keep.tile([P, T + (T - both)], F32, name="fetched")
-        for t0, t1 in ((0, 640), (640, both)):
-            nc.scalar.activation(fetched[:, t0:t1], y[:].indirect(pos2_sb[:, t0 // 16 : t1 // 16]), COPY)
-        nc.scalar.activation(fetched[:, both:T], y[:].indirect(pos1_sb[:, both // 16 :]), COPY)
-        nc.scalar.activation(fetched[:, T:], y[:].indirect(pos2_sb[:, both // 16 :]), COPY)
+        parts = [(0, 512), (512, both)]
+        second = []
+        for i, (t0, t1) in enumerate(parts):
+            second.append(keep.tile([P, t1 - t0], F32, name=f"second{i}"))
+            nc.scalar.activation(second[i][:], y[:].indirect(pos2_sb[:, t0 // 16 : t1 // 16]), COPY)
+        last = keep.tile([P, 2, T - both], F32, name="last")
+        for r, pos_sb in enumerate((pos1_sb, pos2_sb)):
+            nc.scalar.activation(last[:, r, :], y[:].indirect(pos_sb[:, both // 16 :]), COPY)
         first = keep.tile([P, both], F32, name="first")
-        product = keep.tile([P, T + (T - both)], F32, name="product")
-        total = keep.tile([P, T], F32, name="total")
-
-        def multiply(t0, t1):
-            nc.vector.tensor_tensor(product[:, t0:t1], fetched[:, t0:t1], gates[:, 1, t0:t1], MULT)
-
-        def add(t0, t1):
-            nc.vector.tensor_tensor(total[:, t0:t1], first[:, t0:t1], product[:, t0:t1], ADD)
-
-        def store(t0, t1):
-            nc.sync.dma_start(out=out[:, t0:t1], in_=total[:, t0:t1])
-
         nc.vector.tensor_tensor(first[:], y[:].indirect(pos1_sb[:, 0 : both // 16]), gates[:, 0, 0:both], MULT)
-        multiply(0, 384)
-        multiply(384, 640)
-        add(0, 384)
-        store(0, 384)
-        multiply(640, both)
-        add(384, 640)
-        add(640, both)
-        store(384, both)
-        nc.vector.tensor_tensor(
-            product[:, both:].rearrange("p (r t) -> p r t", r=2),
-            fetched[:, both:].rearrange("p (r t) -> p r t", r=2),
-            gates[:, :, both:],
-            MULT,
-        )
-        nc.vector.tensor_tensor(total[:, both:], product[:, both:T], product[:, T:], ADD)
-        store(both, T)
+        product = keep.tile([P, both], F32, name="product")
+        for i, (t0, t1) in enumerate(parts):
+            nc.vector.tensor_tensor(product[:, t0:t1], second[i][:], gates[:, 1, t0:t1], MULT)
+        for i, (t0, t1) in enumerate(parts):
+            total = keep.tile([P, t1 - t0], F32, name=f"total{i}")
+            nc.vector.tensor_tensor(total[:], first[:, t0:t1], product[:, t0:t1], ADD)
+            nc.sync.dma_start(out=out[:, t0:t1], in_=total[:])
+        last_products = keep.tile([P, 2, T - both], F32, name="last_products")
+        nc.vector.tensor_tensor(last_products[:], last[:], gates[:, :, both:], MULT)
+        last_total = keep.tile([P, T - both], F32, name="last_total")
+        nc.vector.tensor_tensor(last_total[:], last_products[:, 0, :], last_products[:, 1, :], ADD)
+        nc.sync.dma_start(out=out[:, both:], in_=last_total[:])

@@ -40,7 +40,7 @@ def tile_routed_moe_kernel(tc, xT, w, gate, offs, pos1, pos2, out):
         x_loads = [(0, 0, 512), (0, 512, 384), (0, 896, 128)]
         x_loads += [(1, 0, 640), (1, 640, 384), (2, 0, 1024)]
         x_calls = [(0, 0, [(256, "v")], [256]), (0, 256, [(256, "s")], [256])]
-        x_calls += [(0, 512, [(320, "v"), (64, "s"), (128, "s")], [256, 256])]
+        x_calls += [(0, 512, [(256, "v"), (128, "s"), (128, "s")], [384, 128])]
         x_calls += [(1, 0, [(384, "s"), (256, "g"), (256, "s"), (128, "g")], [512, 512])]
         x_calls += [(2, 0, [(512, "s"), (128, "s"), (384, "g")], [512, 512])]
         w_chunks = [(0, 4, 0)] + [(u0, 4, 1) for u0 in range(4, 16, 4)] + [(16, 2, 0), (18, 2, 0), (20, 2, 0), (22, 2, 1)]
@@ -77,7 +77,7 @@ def tile_routed_moe_kernel(tc, xT, w, gate, offs, pos1, pos2, out):
         nc.gpsimd.memset(planes[:, 0:T], 0)
 
         def plane_row(a):
-            return 4 * ((a + 1) % PASSES)
+            return 4 * a
 
         def first_word(a):
             return (PASSES - 1 - a) * T

from contextlib import ExitStack

import concourse.mybir as mybir

K, T, E, C, N = 1536, 1024, 8, 256, 128
FLOPS = 2 * K * N * E * C

F32 = mybir.dt.float32
BF16 = mybir.dt.bfloat16
U32 = mybir.dt.uint32
U16 = mybir.dt.uint16
U8 = mybir.dt.uint8
FP8X4 = mybir.dt.float8_e4m3fn_x4
MULT = mybir.AluOpType.mult
ADD = mybir.AluOpType.add
COPY = mybir.ActivationFunctionType.Copy

P = 128
PASSES = K // 512
UNITS = E * PASSES
SLOTS = E * C
WIDE = 2 * SLOTS


def tile_routed_moe_kernel(tc, xT, w, gate, offs, pos1, pos2, out):
    nc = tc.nc
    with ExitStack() as ctx:
        keep = ctx.enter_context(tc.tile_pool(name="keep", bufs=1))
        late = ctx.enter_context(tc.tile_pool(name="late", bufs=1))
        head = ctx.enter_context(tc.tile_pool(name="head", bufs=1))
        psum = ctx.enter_context(tc.psum_pool(name="psum", bufs=1))

        offs_sb = keep.tile([P, E * C // 16], U16, name="offs_sb")
        pos1_sb = keep.tile([P, T // 16], U16, name="pos1_sb")
        pos2_sb = keep.tile([P, T // 16], U16, name="pos2_sb")

        x_view = xT.rearrange("(a p j) n -> a p j n", p=P, j=4)
        w_view = w.rearrange("e (a p j) n -> p e a j n", p=P, j=4)

        x_loads = [(0, 0, 512), (0, 512, 384), (0, 896, 128)]
        x_loads += [(1, 0, 640), (1, 640, 384), (2, 0, 1024)]
        x_calls = [(0, 0, [(256, "v")], [256]), (0, 256, [(256, "s")], [256])]
        x_calls += [(0, 512, [(256, "v"), (128, "s"), (128, "s")], [384, 128])]
        x_calls += [(1, 0, [(384, "s"), (256, "g"), (256, "s"), (128, "g")], [512, 512])]
        x_calls += [(2, 0, [(512, "s"), (128, "s"), (384, "g")], [512, 512])]
        w_chunks = [(0, 4, 0)] + [(u0, 4, 1) for u0 in range(4, 16, 4)] + [(16, 2, 0), (18, 2, 0), (20, 2, 0), (22, 2, 1)]
        units = [(e, 0) for e in range(E)] + [(e, a) for a in (1, 2) for e in range(4)]
        units += [(e, a) for e in range(4, E) for a in (1, 2)]
        w_calls = [[0, 1], [2, 3], [4, 5], [6, 7]]

        x_raw = {}
        for i, (a, t0, n) in enumerate(x_loads):
            raw = keep.tile([P, 4, n], F32, name=f"x_raw{i}")
            nc.sync.dma_start(out=raw[:], in_=x_view[a, :, :, t0 : t0 + n])
            for t in range(t0, t0 + n, 32):
                x_raw[(a, t)] = raw[:, :, t - t0 : n]
            if i == 2:
                nc.sync.dma_start(offs_sb[:], offs)
        w_raw = []
        for i, (u0, n, ng) in enumerate(w_chunks):
            if i == len(w_chunks) - 1:
                raw = late.tile([P, n, 4, N], F32, align_bytes=64, offset=0, name=f"w_raw{i}")
            else:
                raw = keep.tile([P, n, 4, N], F32, align_bytes=64, name=f"w_raw{i}")
            e, a = units[u0]
            src = w_view[:, e : e + n, a, :, :] if n == 4 else w_view[:, e, a : a + n, :, :]
            nc.sync.dma_start(out=raw[:], in_=src)
            w_raw.append(raw)
        nc.sync.dma_start(pos1_sb[:], pos1)
        nc.sync.dma_start(pos2_sb[:], pos2)
        gates = keep.tile([P, 2, T], F32, name="gates")
        for r in range(2):
            nc.sync.dma_start(out=gates[:, r, :], in_=gate[r, :, :])

        words = keep.tile([P, (PASSES - 1) * T + WIDE], U32, align_bytes=64, name="words")
        planes = keep.tile([P, WIDE], U8, align_bytes=64, name="planes")
        nc.gpsimd.memset(planes[:, 0:T], 0)

        def plane_row(a):
            return 4 * a

        def first_word(a):
            return (PASSES - 1 - a) * T

        early_words = keep.tile([P, PASSES - 1, SLOTS], U32, align_bytes=64, name="early_words")
        slot_planes = keep.tile([P, SLOTS], U8, align_bytes=64, name="slot_planes")
        w_codes = keep.tile([P, UNITS, N], U32, align_bytes=64, name="w_codes")
        w_scales = keep.tile([P, UNITS, N], U8, align_bytes=64, name="w_scales")

        def gather(dst, window, s, n):
            nc.vector.tensor_copy(out=dst, in_=window.indirect(offs_sb[:, s // 16 : (s + n) // 16]))

        for k, (a, t0, shares, widths) in enumerate(x_calls):
            n = sum(widths)
            if k in (1, 2):
                grouped = head.tile([P, n * 4], BF16, align_bytes=64, name=f"x_grouped{k}", tag="head")
            else:
                grouped = keep.tile([P, n * 4], BF16, align_bytes=64, name=f"x_grouped{k}")
            t1 = 0
            for m, engine in shares:
                dst = grouped[:, 4 * t1 : 4 * (t1 + m)].rearrange("p (c i j) -> p c j i", i=4, j=4)
                src = x_raw[(a, t0 + t1)][:, :, 0:m].rearrange("p j (c i) -> p c j i", i=4)
                if engine == "v":
                    nc.vector.tensor_copy(out=dst, in_=src)
                elif engine == "s":
                    nc.scalar.copy(out=dst, in_=src)
                else:
                    nc.gpsimd.tensor_copy(
                        out=grouped[:, 4 * t1 : 4 * (t1 + m)].rearrange("p (c j) -> p c j", j=4),
                        in_=x_raw[(a, t0 + t1)][:, :, 0:m].rearrange("p j c -> p c j"),
                    )
                t1 += m
            t1 = 0
            for m in widths:
                nc.vector.quantize_mx(
                    out=words[:, first_word(a) + t0 + t1 : first_word(a) + t0 + t1 + m].bitcast(FP8X4),
                    scales=planes[plane_row(a) : P, t0 + t1 : t0 + t1 + m],
                    in_=grouped[:, 4 * t1 : 4 * (t1 + m)],
                )
                t1 += m
            if t0 + n == T and a < PASSES - 1:
                gather(early_words[:, a, :], words[:, first_word(a) : first_word(a) + WIDE], 0, SLOTS)
        w_grouped = []
        for k, call in enumerate(w_calls):
            grouped = keep.tile(
                [P, sum(w_chunks[i][1] for i in call) * 4 * N], BF16, align_bytes=64, name=f"w_grouped{k}"
            )
            for i in call:
                u0, n, ng = w_chunks[i]
                c0 = (u0 - w_chunks[call[0]][0]) * 4 * N
                ns = n - ng
                nc.scalar.copy(
                    out=grouped[:, c0 : c0 + ns * 4 * N].rearrange("p (u c i j) -> p u c j i", u=ns, i=4, j=4),
                    in_=w_raw[i][:, 0:ns, :, :].rearrange("p u j (c i) -> p u c j i", i=4),
                )
                for u in range(ns, n):
                    nc.gpsimd.tensor_scalar(
                        out=grouped[:, c0 + u * 4 * N : c0 + (u + 1) * 4 * N].rearrange("p (c j) -> p c j", j=4),
                        in0=w_raw[i][:, u, :, :].rearrange("p j c -> p c j"),
                        scalar1=1.0,
                        scalar2=0.0,
                        op0=MULT,
                        op1=ADD,
                    )
            w_grouped.append(grouped)

        def weights(k):
            u0 = w_chunks[w_calls[k][0]][0]
            n = sum(w_chunks[i][1] for i in w_calls[k])
            nc.vector.quantize_mx(
                out=w_codes[:, u0 : u0 + n, :].rearrange("p u n -> p (u n)").bitcast(FP8X4),
                scales=w_scales[:, u0 : u0 + n, :].rearrange("p u n -> p (u n)"),
                in_=w_grouped[k][:],
            )

        gather(slot_planes[:], planes[:], 0, SLOTS)

        last_window = words[:, 0 : 2 * T]
        weights(0)
        late_a = keep.tile([P, 4 * C], U32, align_bytes=64, name="late_a", tag="w_raw1")
        gather(late_a[:], last_window, 0, 4 * C)
        weights(1)
        weights(2)
        late_b = keep.tile([P, 3 * C], U32, align_bytes=64, name="late_b", tag="w_raw5")
        gather(late_b[:], last_window, 4 * C, 3 * C)
        weights(3)
        late_c = late.tile([P, C], U32, align_bytes=64, offset=0, name="late_c")
        gather(late_c[:], last_window, 7 * C, C)
        last_words = [late_a[:, e * C : (e + 1) * C] for e in range(4)]
        last_words += [late_b[:, e * C : (e + 1) * C] for e in range(3)] + [late_c[:]]

        pair = psum.tile([P, 2 * C], F32, name="pair")
        accs = [pair[:, (e - 4) * C : (e - 3) * C] if e in (4, 5) else psum.tile([P, C], F32, name=f"acc{e}")[:] for e in range(E)]
        order = units[:16] + [(e, a) for a in (1, 2) for e in (4, 5)] + units[20:]
        for e, a in order:
            u = units.index((e, a))
            cols = slice(e * C, (e + 1) * C)
            rhs = last_words[e] if a == PASSES - 1 else early_words[:, a, cols]
            nc.tensor.matmul_mx(
                out=accs[e],
                lhsT=w_codes[:, u, :].bitcast(FP8X4),
                lhsT_scale=w_scales[:, u, :],
                rhs=rhs.bitcast(FP8X4),
                rhs_scale=slot_planes[plane_row(a) : P, cols],
                start=(a == 0 and e != 5),
                stop=(a == PASSES - 1 and e != 4),
            )

        y = late.tile([P, SLOTS], F32, align_bytes=64, offset=4 * C, name="y")
        nc.vector.tensor_copy(out=y[:, 4 * C : 6 * C], in_=pair[:])
        for e in range(E):
            if e not in (4, 5):
                nc.scalar.copy(out=y[:, e * C : (e + 1) * C], in_=accs[e])

        both = T - 128
        parts = [(0, 512), (512, both)]
        second = []
        for i, (t0, t1) in enumerate(parts):
            second.append(keep.tile([P, t1 - t0], F32, name=f"second{i}"))
            nc.scalar.activation(second[i][:], y[:].indirect(pos2_sb[:, t0 // 16 : t1 // 16]), COPY)
        last = keep.tile([P, 2, T - both], F32, name="last")
        for r, pos_sb in enumerate((pos1_sb, pos2_sb)):
            nc.scalar.activation(last[:, r, :], y[:].indirect(pos_sb[:, both // 16 :]), COPY)
        first = keep.tile([P, both], F32, name="first")
        nc.vector.tensor_tensor(first[:], y[:].indirect(pos1_sb[:, 0 : both // 16]), gates[:, 0, 0:both], MULT)
        product = keep.tile([P, both], F32, name="product")
        for i, (t0, t1) in enumerate(parts):
            nc.vector.tensor_tensor(product[:, t0:t1], second[i][:], gates[:, 1, t0:t1], MULT)
        for i, (t0, t1) in enumerate(parts):
            total = keep.tile([P, t1 - t0], F32, name=f"total{i}")
            nc.vector.tensor_tensor(total[:], first[:, t0:t1], product[:, t0:t1], ADD)
            nc.sync.dma_start(out=out[:, t0:t1], in_=total[:])
        last_products = keep.tile([P, 2, T - both], F32, name="last_products")
        nc.vector.tensor_tensor(last_products[:], last[:], gates[:, :, both:], MULT)
        last_total = keep.tile([P, T - both], F32, name="last_total")
        nc.vector.tensor_tensor(last_total[:], last_products[:, 0, :], last_products[:, 1, :], ADD)
        nc.sync.dma_start(out=out[:, both:], in_=last_total[:])
